import numpy as np
import ml_dtypes


def mxq(x, axis, fmt="e4m3"):
    dtype, down = {"e4m3": (ml_dtypes.float8_e4m3fn, 7), "e5m2": (ml_dtypes.float8_e5m2, 14)}[fmt]
    v = np.moveaxis(np.asarray(x, np.float32).astype(ml_dtypes.bfloat16).astype(np.float64), axis, -1)
    blocks = v.reshape(v.shape[:-1] + (-1, 32))
    amax = np.abs(blocks).max(-1, keepdims=True)
    byte = np.maximum(np.where(amax > 0, np.frexp(amax)[1] - 1 + 127, 0) - down, 1)
    scale = np.exp2(byte - 127.0)
    codes = (blocks / scale).astype(np.float32).astype(dtype).astype(np.float64)
    return np.moveaxis((codes * scale).reshape(v.shape), -1, axis)


WIDE = False


def mx_kscale(k):
    if not WIDE:
        return np.ones(k)
    levels = np.array([30, -30])
    if k % 512:
        return np.exp2(np.random.permutation(np.resize(levels, k // 32))).repeat(32)
    a = np.empty((k // 512, 16))
    for p in range(k // 512):
        a[p, :8] = np.random.permutation(np.resize(levels, 8))
        for g in range(8):
            far = levels[np.abs(levels - a[p, g]) >= 10]
            a[p, g + 8] = far[np.random.randint(len(far))]
    return np.exp2(a.ravel()).repeat(32)


def f64(x):
    return np.asarray(x).astype(np.float64)


def striped(idx):
    return np.tile(np.asarray(idx).reshape(-1, 16).T, (8, 1)).astype(np.uint16)


def unstriped(offs):
    return offs[:16].T.reshape(-1).astype(np.int64)


def bf(x):
    return np.asarray(x, np.float32).astype(ml_dtypes.bfloat16)


def planes(Y):
    r, m = Y.shape
    b = f64(bf(Y)).reshape(r // 32, 32, m)
    amax = np.abs(b).max(1)
    byte = np.clip(np.where(amax > 0, np.frexp(amax)[1] - 1 + 127 - 7, 1), 1, 254)
    codes = (b * np.exp2(127.0 - byte)[:, None, :]).reshape(r, m).astype(np.float32).astype(ml_dtypes.float8_e4m3fn).view(np.uint8)
    words = codes.reshape(r // 512, 128, 4, m).transpose(0, 1, 3, 2)
    return np.ascontiguousarray(words), np.ascontiguousarray(byte.astype(np.uint8).reshape(r // 512, 16, m))


K, N, T, J = 512, 512, 1024, 512


def setup_inputs():
    n = np.random.standard_normal
    idx = np.random.permutation(T)[:J]
    fj = mx_kscale(J)
    tj = np.ones(T)
    tj[idx] = fj
    return {
        "xt": (n((K, T)) * tj).astype(np.float32),
        "g": (n((N, T)) * np.exp(0.5 * n((1, T)))).astype(np.float32),
        "sv": (n((N, T))).astype(np.float32),
        "rb": (np.random.uniform(0.4, 1.2, (1, J)) / fj).astype(np.float32),
        "mom": (1.0 * n((K, N))).astype(np.float32),
        "offs": striped(idx),
    }


def reference(xt, g, sv, rb, mom, offs):
    idx = unstriped(offs)
    xj = f64(xt)[:, idx].T
    gs = f64(g)[:, idx] * f64(sv)[:, idx] * f64(rb)
    gj = gs.T
    xjq = mxq(xj, 0, "e4m3")
    gjq = mxq(gj, 0, "e5m2")
    w = xjq.T @ gjq
    y = 0.04 * w + 0.5 * f64(mom)
    words, scales = planes(y)
    return y, words, scales

@@ -1,0 +1,182 @@
+from contextlib import ExitStack
+
+import concourse.mybir as mybir
+from concourse.masks import make_identity
+
+K, N, T, J = 512, 512, 1024, 512
+FLOPS = 2 * K * N * J
+F32 = mybir.dt.float32
+BF16 = mybir.dt.bfloat16
+U32 = mybir.dt.uint32
+I32 = mybir.dt.int32
+U16 = mybir.dt.uint16
+U8 = mybir.dt.uint8
+E4M3 = mybir.dt.float8_e4m3fn_x4
+E5M2 = mybir.dt.float8_e5m2_x4
+MULT = mybir.AluOpType.mult
+ADD = mybir.AluOpType.add
+COPY = mybir.ActivationFunctionType.Copy
+P = 128
+ORDER = ["g0","g1","s0","s1","x0","g2","g3","s2","x1","s3","x2","x3","m0","m1","m2","m3"]
+SPLIT = 352
+
+
+def tile_moe_expert_wgrad_through_saved_pl_kernel(tc, xt, g, sv, rb, mom, offs, out_0, out_1, out_2):
+    nc = tc.nc
+    with ExitStack() as ctx:
+        keep = ctx.enter_context(tc.tile_pool(name="keep", bufs=1))
+        tail = ctx.enter_context(tc.tile_pool(name="tail", bufs=1))
+        psum = ctx.enter_context(tc.psum_pool(name="psum", bufs=1))
+
+        rb_col = keep.tile([P, 4], F32, name="rb_col")
+        nc.sync.dma_start(rb_col[:], rb.rearrange("o (p t) -> p (o t)", t=4))
+        offsets = keep.tile([P, J // 16], U16, name="offsets")
+        nc.sync.dma_start(offsets[:], offs)
+
+        x_rows = xt.rearrange("(p t) c -> p t c", t=4)
+        mom_rows = mom.rearrange("(p t) n -> p t n", t=4)
+        out_rows = out_0.rearrange("(p t) n -> p t n", t=4)
+        raw = {}
+        for name in ORDER:
+            i = int(name[1])
+            width = N if name[0] == "m" else T
+            raw[name] = keep.tile([P, width], F32, name="raw_" + name, align_bytes=64)
+            src = {"g": g[P * i : P * (i + 1), :], "s": sv[P * i : P * (i + 1), :], "x": x_rows[:, i, :], "m": mom_rows[:, i, :]}[name[0]]
+            nc.sync.dma_start(raw[name][:], src)
+
+        ident = keep.tile([P, P], F32, name="ident")
+        make_identity(nc, ident[:])
+
+        def sb(shape, dtype, tag):
+            return keep.tile(shape, dtype, name=tag, tag=tag, align_bytes=64)
+
+        def bank(tag):
+            return psum.tile([P, 4, P], F32, name=tag, tag=tag)
+
+        rb_bank = bank("b0")
+        for t in range(4):
+            nc.tensor.transpose(rb_bank[:, t, :], rb_col[:, t : t + 1].to_broadcast([P, P]), ident[:])
+        rb_all = sb([P, J], F32, "rb_all")
+        nc.vector.tensor_copy(rb_all[:].rearrange("m (p t) -> m p t", t=4), rb_bank[:].rearrange("m t p -> m p t"))
+
+        g_codes = sb([P, N], U32, "g_codes")
+        g_scales = sb([P, N], U8, "g_scales")
+        x0_codes = sb([P, P], U32, "x0_codes")
+        x0_scales = sb([P, P], U8, "x0_scales")
+        x12_codes = sb([P, 2 * P], U32, "x12_codes")
+        x12_scales = sb([P, 2 * P], U8, "x12_scales")
+        x3_scales = sb([P, P], U8, "x3_scales")
+
+        def gather_x_on_scalar(i, narrow_tag):
+            narrow = sb([P, T], BF16, narrow_tag)
+            nc.scalar.copy(narrow[:], raw["x%d" % i][:])
+            picked = sb([P, J], BF16, "x_picked%d" % i)
+            nc.scalar.activation(picked[:], narrow[:].indirect(offsets[:]), COPY)
+            return picked
+
+        def turn_pairs(picked, bank_tag):
+            words = picked[:].bitcast(F32)
+            turned = bank(bank_tag)
+            for u in range(2):
+                nc.tensor.transpose(turned[:, u, :], words[:, u::2], ident[:])
+            return turned
+
+        def group_pairs(grouped, turned):
+            nc.scalar.copy(grouped.bitcast(F32).rearrange("p (c u) -> p c u", u=2), turned[:, 0:2, :].rearrange("p u c -> p c u"))
+
+        def gather_g(i):
+            weighted = sb([P, J], F32, "weighted%d" % i)
+            nc.vector.tensor_tensor(weighted[:], raw["g%d" % i][:].indirect(offsets[:]), rb_all[:], MULT)
+            return weighted
+
+        def gather_s(i, weighted, gs_tag):
+            gs = sb([P, J], F32, gs_tag)
+            nc.vector.tensor_tensor(gs[:], raw["s%d" % i][:].indirect(offsets[:]), weighted[:], MULT)
+            return gs
+
+        def turn_gs(gs, bank_tag):
+            turned = bank(bank_tag)
+            for t in range(4):
+                nc.tensor.transpose(turned[:, t, :], gs[:, t::4], ident[:])
+            return turned
+
+        def group_gs(grouped, turned):
+            nc.scalar.copy(grouped.rearrange("p (c t) -> p c t", t=4), turned[:].rearrange("p t c -> p c t"))
+
+        def quantize(codes, scales, fmt, first, grouped):
+            cols = slice(P * first, P * first + grouped.shape[1] // 4)
+            nc.vector.quantize_mx(out=codes[:, cols].bitcast(fmt), scales=scales[:, cols], in_=grouped)
+
+        early = sb([P, 3 * J], BF16, "early")
+        w0 = gather_g(0)
+        w1 = gather_g(1)
+        g0_turned = turn_gs(gather_s(0, w0, "gs0"), "b0")
+        g1_turned = turn_gs(gather_s(1, w1, "gs1"), "b2")
+        x0_picked = gather_x_on_scalar(0, "narrow")
+        group_gs(early[:, 0:J], g0_turned)
+        group_gs(early[:, J : 2 * J], g1_turned)
+        group_pairs(early[:, 2 * J : 3 * J], turn_pairs(x0_picked, "b0"))
+        w2 = gather_g(2)
+        w3 = gather_g(3)
+        g2_turned = turn_gs(gather_s(2, w2, "gs2"), "b3")
+        quantize(x0_codes, x0_scales, E4M3, 0, early[:, 2 * J : 3 * J])
+        quantize(g_codes, g_scales, E5M2, 0, early[:, 0 : 2 * J])
+        x1_turned = turn_pairs(gather_x_on_scalar(1, "raw_g3"), "b1")
+        gs3 = gather_s(3, w3, "early")
+        g3_dealt = sb([P, J], BF16, "raw_g3")
+        g3_turned = bank("b2")
+        for u in range(2):
+            half_cols = slice(2 * P * u, 2 * P * (u + 1))
+            nc.scalar.copy(g3_dealt[:, half_cols].rearrange("p (q e) -> p q e", e=2), gs3[:].rearrange("p (q u e) -> p u q e", u=2, e=2)[:, u])
+            nc.tensor.transpose(g3_turned[:, u, :], g3_dealt[:, half_cols].bitcast(F32), ident[:])
+        g23_grouped = sb([P, 2 * J], BF16, "early")
+        group_gs(g23_grouped[:, 0:J], g2_turned)
+        group_pairs(g23_grouped[:, J : 2 * J], g3_turned)
+        x12_grouped = sb([P, 2 * J], BF16, "raw_g3")
+        group_pairs(x12_grouped[:, 0:J], x1_turned)
+
+        x2_picked = sb([P, J], BF16, "x_picked2")
+        nc.vector.tensor_copy(x2_picked[:], raw["x2"][:].indirect(offsets[:]))
+        group_pairs(x12_grouped[:, J : 2 * J], turn_pairs(x2_picked, "b3"))
+        x3_picked = sb([P, J], BF16, "x_picked3")
+        nc.vector.tensor_copy(x3_picked[:], raw["x3"][:].indirect(offsets[:]))
+        x3_grouped = tail.tile([P, J], BF16, name="x3_grouped", align_bytes=64, offset=16 * N - J)
+        group_pairs(x3_grouped[:], turn_pairs(x3_picked, "b1"))
+
+        quantize(g_codes, g_scales, E5M2, 2, g23_grouped[:])
+        quantize(x12_codes, x12_scales, E4M3, 0, x12_grouped[:])
+        half = [sb([P, N], F32, "raw_g3"), sb([P, N], F32, "raw_m0")]
+        for t in range(2):
+            nc.vector.tensor_scalar_mul(half[t][:], raw["m%d" % t][:], 0.5)
+        x3_codes = sb([P, P], U32, "raw_m1")
+        nc.vector.quantize_mx(out=x3_codes[:].bitcast(E4M3), scales=x3_scales[:], in_=x3_grouped[:])
+        half = half + [tail.tile([P, N], F32, name="half2", offset=16 * N), sb([P, N], F32, "raw_m2")]
+        for t in range(2, 4):
+            nc.scalar.activation(half[t][:], raw["m%d" % t][:], COPY, scale=0.5)
+
+        y = tail.tile([P, 4, N], F32, name="y", offset=0)
+        H = N // 2
+        for t in range(4):
+            acc = psum.tile([P, N], F32, name="acc%d" % t)
+            codes, scales = [(x0_codes[:], x0_scales[:]), (x12_codes[:, :P], x12_scales[:, :P]), (x12_codes[:, P:], x12_scales[:, P:]), (x3_codes[:], x3_scales[:])][t]
+            nc.tensor.matmul_mx(out=acc[:], lhsT=codes.bitcast(E4M3), lhsT_scale=scales,
+                                rhs=g_codes[:].bitcast(E5M2), rhs_scale=g_scales[:], start=True, stop=True)
+            for part in ([slice(H, N), slice(0, H)] if t == 3 else [slice(0, N)]):
+                nc.vector.scalar_tensor_tensor(y[:, t, part], acc[:, part], 0.04, half[t][:, part], MULT, ADD)
+            nc.sync.dma_start(out_rows[:, t, :], y[:, t, :])
+
+        y_turned = y[:].rearrange("p t n -> p n t")
+        y_lo = sb([P, H, 4], BF16, "y_lo")
+        y_hi = sb([P, H, 4], BF16, "y_hi")
+        nc.scalar.copy(y_hi[:, SPLIT - H :, :], y_turned[:, SPLIT:, :])
+        nc.vector.tensor_copy(y_hi[:, : SPLIT - H, :], y_turned[:, H:SPLIT, :])
+        nc.vector.tensor_copy(y_lo[:], y_turned[:, :H, :])
+        y_codes = sb([P, N], U32, "y_codes")
+        y_scales = sb([P, N], U8, "y_scales")
+        words_out = out_1[0].rearrange("p c r -> p (c r)").bitcast(I32)
+        for part, grouped in ((slice(H, N), y_hi), (slice(0, H), y_lo)):
+            nc.vector.quantize_mx(out=y_codes[:, part].bitcast(E4M3), scales=y_scales[:, part], in_=grouped[:].rearrange("p n t -> p (n t)"))
+            nc.sync.dma_start(words_out[:, part], y_codes[:, part].bitcast(I32))
+        for q in range(4):
+            queue = nc.sync if q % 2 else nc.scalar
+            queue.dma_start(out_2[0, 4 * q : 4 * q + 4, :].bitcast(I32), y_scales[32 * q : 32 * q + 4, :].bitcast(I32))

@@ -17,7 +17,7 @@ MULT = mybir.AluOpType.mult
 ADD = mybir.AluOpType.add
 COPY = mybir.ActivationFunctionType.Copy
 P = 128
-ORDER = ["g0","g1","s0","s1","x0","g2","g3","s2","x1","s3","x2","x3","m0","m1","m2","m3"]
+ORDER = ["g0","g1","s0","s1","x0","g2","g3","s2","x1","s3","x2","x3","m0","m1"]
 SPLIT = 352
 
 
@@ -25,7 +25,6 @@ def tile_moe_expert_wgrad_through_saved_pl_kernel(tc, xt, g, sv, rb, mom, offs, 
     nc = tc.nc
     with ExitStack() as ctx:
         keep = ctx.enter_context(tc.tile_pool(name="keep", bufs=1))
-        tail = ctx.enter_context(tc.tile_pool(name="tail", bufs=1))
         psum = ctx.enter_context(tc.psum_pool(name="psum", bufs=1))
 
         rb_col = keep.tile([P, 4], F32, name="rb_col")
@@ -39,9 +38,9 @@ def tile_moe_expert_wgrad_through_saved_pl_kernel(tc, xt, g, sv, rb, mom, offs, 
         raw = {}
         for name in ORDER:
             i = int(name[1])
-            width = N if name[0] == "m" else T
-            raw[name] = keep.tile([P, width], F32, name="raw_" + name, align_bytes=64)
-            src = {"g": g[P * i : P * (i + 1), :], "s": sv[P * i : P * (i + 1), :], "x": x_rows[:, i, :], "m": mom_rows[:, i, :]}[name[0]]
+            shape = [P, 2, N] if name[0] == "m" else [P, T]
+            raw[name] = keep.tile(shape, F32, name="raw_" + name, align_bytes=64)
+            src = {"g": g[P * i : P * (i + 1), :], "s": sv[P * i : P * (i + 1), :], "x": x_rows[:, i, :], "m": mom_rows[:, 2 * (i % 2) : 2 * (i % 2) + 2, :]}[name[0]]
             nc.sync.dma_start(raw[name][:], src)
 
         ident = keep.tile([P, P], F32, name="ident")
@@ -140,21 +139,21 @@ def tile_moe_expert_wgrad_through_saved_pl_kernel(tc, xt, g, sv, rb, mom, offs, 
         group_pairs(x12_grouped[:, J : 2 * J], turn_pairs(x2_picked, "b3"))
         x3_picked = sb([P, J], BF16, "x_picked3")
         nc.vector.tensor_copy(x3_picked[:], raw["x3"][:].indirect(offsets[:]))
-        x3_grouped = tail.tile([P, J], BF16, name="x3_grouped", align_bytes=64, offset=16 * N - J)
+        x3_grouped = sb([P, J], BF16, "x3_grouped")
         group_pairs(x3_grouped[:], turn_pairs(x3_picked, "b1"))
 
         quantize(g_codes, g_scales, E5M2, 2, g23_grouped[:])
         quantize(x12_codes, x12_scales, E4M3, 0, x12_grouped[:])
-        half = [sb([P, N], F32, "raw_g3"), sb([P, N], F32, "raw_m0")]
-        for t in range(2):
-            nc.vector.tensor_scalar_mul(half[t][:], raw["m%d" % t][:], 0.5)
-        x3_codes = sb([P, P], U32, "raw_m1")
+        half01 = sb([P, 2, N], F32, "early")
+        nc.vector.tensor_scalar_mul(half01[:], raw["m0"][:], 0.5)
+        x3_codes = sb([P, P], U32, "x3_codes")
         nc.vector.quantize_mx(out=x3_codes[:].bitcast(E4M3), scales=x3_scales[:], in_=x3_grouped[:])
-        half = half + [tail.tile([P, N], F32, name="half2", offset=16 * N), sb([P, N], F32, "raw_m2")]
-        for t in range(2, 4):
-            nc.scalar.activation(half[t][:], raw["m%d" % t][:], COPY, scale=0.5)
+        half23 = sb([P, 2, N], F32, "x_picked3")
+        for t in range(2):
+            nc.scalar.activation(half23[:, t, :], raw["m1"][:, t, :], COPY, scale=0.5)
+        half = [half01[:, 0, :], half01[:, 1, :], half23[:, 0, :], half23[:, 1, :]]
 
-        y = tail.tile([P, 4, N], F32, name="y", offset=0)
+        y = sb([P, 4, N], F32, "y")
         H = N // 2
         for t in range(4):
             acc = psum.tile([P, N], F32, name="acc%d" % t)
@@ -165,12 +164,16 @@ def tile_moe_expert_wgrad_through_saved_pl_kernel(tc, xt, g, sv, rb, mom, offs, 
                 nc.vector.scalar_tensor_tensor(y[:, t, part], acc[:, part], 0.04, half[t][:, part], MULT, ADD)
             nc.sync.dma_start(out_rows[:, t, :], y[:, t, :])
 
-        y_turned = y[:].rearrange("p t n -> p n t")
         y_lo = sb([P, H, 4], BF16, "y_lo")
         y_hi = sb([P, H, 4], BF16, "y_hi")
-        nc.scalar.copy(y_hi[:, SPLIT - H :, :], y_turned[:, SPLIT:, :])
-        nc.vector.tensor_copy(y_hi[:, : SPLIT - H, :], y_turned[:, H:SPLIT, :])
-        nc.vector.tensor_copy(y_lo[:], y_turned[:, :H, :])
+
+        def views(grouped, first, cols):
+            dst = grouped[:, cols.start - first : cols.stop - first, :].rearrange("p (c i) t -> p c t i", i=4)
+            return dst, y[:, :, cols].rearrange("p t (c i) -> p c t i", i=4)
+
+        nc.scalar.copy(*views(y_hi, H, slice(SPLIT, N)))
+        nc.vector.tensor_copy(*views(y_hi, H, slice(H, SPLIT)))
+        nc.vector.tensor_copy(*views(y_lo, 0, slice(0, H)))
         y_codes = sb([P, N], U32, "y_codes")
         y_scales = sb([P, N], U8, "y_scales")
         words_out = out_1[0].rearrange("p c r -> p (c r)").bitcast(I32)

@@ -17,7 +17,7 @@ MULT = mybir.AluOpType.mult
 ADD = mybir.AluOpType.add
 COPY = mybir.ActivationFunctionType.Copy
 P = 128
-ORDER = ["g0","g1","s0","s1","x0","g2","g3","s2","x1","s3","x2","x3","m0","m1"]
+ORDER = ["g0","g1","x0","s0","s1","g2","g3","x1","s2","s3","x2","x3","m0","m1"]
 SPLIT = 352
 
 
@@ -28,9 +28,8 @@ def tile_moe_expert_wgrad_through_saved_pl_kernel(tc, xt, g, sv, rb, mom, offs, 
         psum = ctx.enter_context(tc.psum_pool(name="psum", bufs=1))
 
         rb_col = keep.tile([P, 4], F32, name="rb_col")
-        nc.sync.dma_start(rb_col[:], rb.rearrange("o (p t) -> p (o t)", t=4))
+        nc.scalar.dma_start(rb_col[:], rb.rearrange("o (p t) -> p (o t)", t=4))
         offsets = keep.tile([P, J // 16], U16, name="offsets")
-        nc.sync.dma_start(offsets[:], offs)
 
         x_rows = xt.rearrange("(p t) c -> p t c", t=4)
         mom_rows = mom.rearrange("(p t) n -> p t n", t=4)
@@ -42,6 +41,8 @@ def tile_moe_expert_wgrad_through_saved_pl_kernel(tc, xt, g, sv, rb, mom, offs, 
             raw[name] = keep.tile(shape, F32, name="raw_" + name, align_bytes=64)
             src = {"g": g[P * i : P * (i + 1), :], "s": sv[P * i : P * (i + 1), :], "x": x_rows[:, i, :], "m": mom_rows[:, 2 * (i % 2) : 2 * (i % 2) + 2, :]}[name[0]]
             nc.sync.dma_start(raw[name][:], src)
+            if name == ORDER[0]:
+                nc.sync.dma_start(offsets[:], offs)
 
         ident = keep.tile([P, P], F32, name="ident")
         make_identity(nc, ident[:])
@@ -109,26 +110,23 @@ def tile_moe_expert_wgrad_through_saved_pl_kernel(tc, xt, g, sv, rb, mom, offs, 
         early = sb([P, 3 * J], BF16, "early")
         w0 = gather_g(0)
         w1 = gather_g(1)
-        g0_turned = turn_gs(gather_s(0, w0, "gs0"), "b0")
-        g1_turned = turn_gs(gather_s(1, w1, "gs1"), "b2")
-        x0_picked = gather_x_on_scalar(0, "narrow")
-        group_gs(early[:, 0:J], g0_turned)
-        group_gs(early[:, J : 2 * J], g1_turned)
-        group_pairs(early[:, 2 * J : 3 * J], turn_pairs(x0_picked, "b0"))
+        group_pairs(early[:, 2 * J : 3 * J], turn_pairs(gather_x_on_scalar(0, "narrow"), "b1"))
+        group_gs(early[:, 0:J], turn_gs(gather_s(0, w0, "gs0"), "b0"))
+        group_gs(early[:, J : 2 * J], turn_gs(gather_s(1, w1, "gs1"), "b2"))
         w2 = gather_g(2)
         w3 = gather_g(3)
-        g2_turned = turn_gs(gather_s(2, w2, "gs2"), "b3")
         quantize(x0_codes, x0_scales, E4M3, 0, early[:, 2 * J : 3 * J])
         quantize(g_codes, g_scales, E5M2, 0, early[:, 0 : 2 * J])
+        g2_turned = turn_gs(gather_s(2, w2, "early"), "b3")
         x1_turned = turn_pairs(gather_x_on_scalar(1, "raw_g3"), "b1")
-        gs3 = gather_s(3, w3, "early")
+        gs3 = gather_s(3, w3, "gs3")
         g3_dealt = sb([P, J], BF16, "raw_g3")
         g3_turned = bank("b2")
         for u in range(2):
             half_cols = slice(2 * P * u, 2 * P * (u + 1))
             nc.scalar.copy(g3_dealt[:, half_cols].rearrange("p (q e) -> p q e", e=2), gs3[:].rearrange("p (q u e) -> p u q e", u=2, e=2)[:, u])
             nc.tensor.transpose(g3_turned[:, u, :], g3_dealt[:, half_cols].bitcast(F32), ident[:])
-        g23_grouped = sb([P, 2 * J], BF16, "early")
+        g23_grouped = sb([P, 2 * J], BF16, "gs3")
         group_gs(g23_grouped[:, 0:J], g2_turned)
         group_pairs(g23_grouped[:, J : 2 * J], g3_turned)
         x12_grouped = sb([P, 2 * J], BF16, "raw_g3")
@@ -144,7 +142,7 @@ def tile_moe_expert_wgrad_through_saved_pl_kernel(tc, xt, g, sv, rb, mom, offs, 
 
         quantize(g_codes, g_scales, E5M2, 2, g23_grouped[:])
         quantize(x12_codes, x12_scales, E4M3, 0, x12_grouped[:])
-        half01 = sb([P, 2, N], F32, "early")
+        half01 = sb([P, 2, N], F32, "gs3")
         nc.vector.tensor_scalar_mul(half01[:], raw["m0"][:], 0.5)
         x3_codes = sb([P, P], U32, "x3_codes")
         nc.vector.quantize_mx(out=x3_codes[:].bitcast(E4M3), scales=x3_scales[:], in_=x3_grouped[:])

@@ -28,7 +28,7 @@ def tile_moe_expert_wgrad_through_saved_pl_kernel(tc, xt, g, sv, rb, mom, offs, 
         psum = ctx.enter_context(tc.psum_pool(name="psum", bufs=1))
 
         rb_col = keep.tile([P, 4], F32, name="rb_col")
-        nc.scalar.dma_start(rb_col[:], rb.rearrange("o (p t) -> p (o t)", t=4))
+        nc.sync.dma_start(rb_col[:], rb.rearrange("o (p t) -> p (o t)", t=4))
         offsets = keep.tile([P, J // 16], U16, name="offsets")
 
         x_rows = xt.rearrange("(p t) c -> p t c", t=4)

from contextlib import ExitStack

import concourse.mybir as mybir
from concourse.masks import make_identity

K, N, T, J = 512, 512, 1024, 512
FLOPS = 2 * K * N * J
F32 = mybir.dt.float32
BF16 = mybir.dt.bfloat16
U32 = mybir.dt.uint32
I32 = mybir.dt.int32
U16 = mybir.dt.uint16
U8 = mybir.dt.uint8
E4M3 = mybir.dt.float8_e4m3fn_x4
E5M2 = mybir.dt.float8_e5m2_x4
MULT = mybir.AluOpType.mult
ADD = mybir.AluOpType.add
COPY = mybir.ActivationFunctionType.Copy
P = 128
ORDER = ["g0","g1","x0","s0","s1","g2","g3","x1","s2","s3","x2","x3","m0","m1"]
SPLIT = 352


def tile_moe_expert_wgrad_through_saved_pl_kernel(tc, xt, g, sv, rb, mom, offs, out_0, out_1, out_2):
    nc = tc.nc
    with ExitStack() as ctx:
        keep = ctx.enter_context(tc.tile_pool(name="keep", bufs=1))
        psum = ctx.enter_context(tc.psum_pool(name="psum", bufs=1))

        rb_col = keep.tile([P, 4], F32, name="rb_col")
        nc.sync.dma_start(rb_col[:], rb.rearrange("o (p t) -> p (o t)", t=4))
        offsets = keep.tile([P, J // 16], U16, name="offsets")

        x_rows = xt.rearrange("(p t) c -> p t c", t=4)
        mom_rows = mom.rearrange("(p t) n -> p t n", t=4)
        out_rows = out_0.rearrange("(p t) n -> p t n", t=4)
        raw = {}
        for name in ORDER:
            i = int(name[1])
            shape = [P, 2, N] if name[0] == "m" else [P, T]
            raw[name] = keep.tile(shape, F32, name="raw_" + name, align_bytes=64)
            src = {"g": g[P * i : P * (i + 1), :], "s": sv[P * i : P * (i + 1), :], "x": x_rows[:, i, :], "m": mom_rows[:, 2 * (i % 2) : 2 * (i % 2) + 2, :]}[name[0]]
            nc.sync.dma_start(raw[name][:], src)
            if name == ORDER[0]:
                nc.sync.dma_start(offsets[:], offs)

        ident = keep.tile([P, P], F32, name="ident")
        make_identity(nc, ident[:])

        def sb(shape, dtype, tag):
            return keep.tile(shape, dtype, name=tag, tag=tag, align_bytes=64)

        def bank(tag):
            return psum.tile([P, 4, P], F32, name=tag, tag=tag)

        rb_bank = bank("b0")
        for t in range(4):
            nc.tensor.transpose(rb_bank[:, t, :], rb_col[:, t : t + 1].to_broadcast([P, P]), ident[:])
        rb_all = sb([P, J], F32, "rb_all")
        nc.vector.tensor_copy(rb_all[:].rearrange("m (p t) -> m p t", t=4), rb_bank[:].rearrange("m t p -> m p t"))

        g_codes = sb([P, N], U32, "g_codes")
        g_scales = sb([P, N], U8, "g_scales")
        x0_codes = sb([P, P], U32, "x0_codes")
        x0_scales = sb([P, P], U8, "x0_scales")
        x12_codes = sb([P, 2 * P], U32, "x12_codes")
        x12_scales = sb([P, 2 * P], U8, "x12_scales")
        x3_scales = sb([P, P], U8, "x3_scales")

        def gather_x_on_scalar(i, narrow_tag):
            narrow = sb([P, T], BF16, narrow_tag)
            nc.scalar.copy(narrow[:], raw["x%d" % i][:])
            picked = sb([P, J], BF16, "x_picked%d" % i)
            nc.scalar.activation(picked[:], narrow[:].indirect(offsets[:]), COPY)
            return picked

        def turn_pairs(picked, bank_tag):
            words = picked[:].bitcast(F32)
            turned = bank(bank_tag)
            for u in range(2):
                nc.tensor.transpose(turned[:, u, :], words[:, u::2], ident[:])
            return turned

        def group_pairs(grouped, turned):
            nc.scalar.copy(grouped.bitcast(F32).rearrange("p (c u) -> p c u", u=2), turned[:, 0:2, :].rearrange("p u c -> p c u"))

        def gather_g(i):
            weighted = sb([P, J], F32, "weighted%d" % i)
            nc.vector.tensor_tensor(weighted[:], raw["g%d" % i][:].indirect(offsets[:]), rb_all[:], MULT)
            return weighted

        def gather_s(i, weighted, gs_tag):
            gs = sb([P, J], F32, gs_tag)
            nc.vector.tensor_tensor(gs[:], raw["s%d" % i][:].indirect(offsets[:]), weighted[:], MULT)
            return gs

        def turn_gs(gs, bank_tag):
            turned = bank(bank_tag)
            for t in range(4):
                nc.tensor.transpose(turned[:, t, :], gs[:, t::4], ident[:])
            return turned

        def group_gs(grouped, turned):
            nc.scalar.copy(grouped.rearrange("p (c t) -> p c t", t=4), turned[:].rearrange("p t c -> p c t"))

        def quantize(codes, scales, fmt, first, grouped):
            cols = slice(P * first, P * first + grouped.shape[1] // 4)
            nc.vector.quantize_mx(out=codes[:, cols].bitcast(fmt), scales=scales[:, cols], in_=grouped)

        early = sb([P, 3 * J], BF16, "early")
        w0 = gather_g(0)
        w1 = gather_g(1)
        group_pairs(early[:, 2 * J : 3 * J], turn_pairs(gather_x_on_scalar(0, "narrow"), "b1"))
        group_gs(early[:, 0:J], turn_gs(gather_s(0, w0, "gs0"), "b0"))
        group_gs(early[:, J : 2 * J], turn_gs(gather_s(1, w1, "gs1"), "b2"))
        w2 = gather_g(2)
        w3 = gather_g(3)
        quantize(x0_codes, x0_scales, E4M3, 0, early[:, 2 * J : 3 * J])
        quantize(g_codes, g_scales, E5M2, 0, early[:, 0 : 2 * J])
        g2_turned = turn_gs(gather_s(2, w2, "early"), "b3")
        x1_turned = turn_pairs(gather_x_on_scalar(1, "raw_g3"), "b1")
        gs3 = gather_s(3, w3, "gs3")
        g3_dealt = sb([P, J], BF16, "raw_g3")
        g3_turned = bank("b2")
        for u in range(2):
            half_cols = slice(2 * P * u, 2 * P * (u + 1))
            nc.scalar.copy(g3_dealt[:, half_cols].rearrange("p (q e) -> p q e", e=2), gs3[:].rearrange("p (q u e) -> p u q e", u=2, e=2)[:, u])
            nc.tensor.transpose(g3_turned[:, u, :], g3_dealt[:, half_cols].bitcast(F32), ident[:])
        g23_grouped = sb([P, 2 * J], BF16, "gs3")
        group_gs(g23_grouped[:, 0:J], g2_turned)
        group_pairs(g23_grouped[:, J : 2 * J], g3_turned)
        x12_grouped = sb([P, 2 * J], BF16, "raw_g3")
        group_pairs(x12_grouped[:, 0:J], x1_turned)

        x2_picked = sb([P, J], BF16, "x_picked2")
        nc.vector.tensor_copy(x2_picked[:], raw["x2"][:].indirect(offsets[:]))
        group_pairs(x12_grouped[:, J : 2 * J], turn_pairs(x2_picked, "b3"))
        x3_picked = sb([P, J], BF16, "x_picked3")
        nc.vector.tensor_copy(x3_picked[:], raw["x3"][:].indirect(offsets[:]))
        x3_grouped = sb([P, J], BF16, "x3_grouped")
        group_pairs(x3_grouped[:], turn_pairs(x3_picked, "b1"))

        quantize(g_codes, g_scales, E5M2, 2, g23_grouped[:])
        quantize(x12_codes, x12_scales, E4M3, 0, x12_grouped[:])
        half01 = sb([P, 2, N], F32, "gs3")
        nc.vector.tensor_scalar_mul(half01[:], raw["m0"][:], 0.5)
        x3_codes = sb([P, P], U32, "x3_codes")
        nc.vector.quantize_mx(out=x3_codes[:].bitcast(E4M3), scales=x3_scales[:], in_=x3_grouped[:])
        half23 = sb([P, 2, N], F32, "x_picked3")
        for t in range(2):
            nc.scalar.activation(half23[:, t, :], raw["m1"][:, t, :], COPY, scale=0.5)
        half = [half01[:, 0, :], half01[:, 1, :], half23[:, 0, :], half23[:, 1, :]]

        y = sb([P, 4, N], F32, "y")
        H = N // 2
        for t in range(4):
            acc = psum.tile([P, N], F32, name="acc%d" % t)
            codes, scales = [(x0_codes[:], x0_scales[:]), (x12_codes[:, :P], x12_scales[:, :P]), (x12_codes[:, P:], x12_scales[:, P:]), (x3_codes[:], x3_scales[:])][t]
            nc.tensor.matmul_mx(out=acc[:], lhsT=codes.bitcast(E4M3), lhsT_scale=scales,
                                rhs=g_codes[:].bitcast(E5M2), rhs_scale=g_scales[:], start=True, stop=True)
            for part in ([slice(H, N), slice(0, H)] if t == 3 else [slice(0, N)]):
                nc.vector.scalar_tensor_tensor(y[:, t, part], acc[:, part], 0.04, half[t][:, part], MULT, ADD)
            nc.sync.dma_start(out_rows[:, t, :], y[:, t, :])

        y_lo = sb([P, H, 4], BF16, "y_lo")
        y_hi = sb([P, H, 4], BF16, "y_hi")

        def views(grouped, first, cols):
            dst = grouped[:, cols.start - first : cols.stop - first, :].rearrange("p (c i) t -> p c t i", i=4)
            return dst, y[:, :, cols].rearrange("p t (c i) -> p c t i", i=4)

        nc.scalar.copy(*views(y_hi, H, slice(SPLIT, N)))
        nc.vector.tensor_copy(*views(y_hi, H, slice(H, SPLIT)))
        nc.vector.tensor_copy(*views(y_lo, 0, slice(0, H)))
        y_codes = sb([P, N], U32, "y_codes")
        y_scales = sb([P, N], U8, "y_scales")
        words_out = out_1[0].rearrange("p c r -> p (c r)").bitcast(I32)
        for part, grouped in ((slice(H, N), y_hi), (slice(0, H), y_lo)):
            nc.vector.quantize_mx(out=y_codes[:, part].bitcast(E4M3), scales=y_scales[:, part], in_=grouped[:].rearrange("p n t -> p (n t)"))
            nc.sync.dma_start(words_out[:, part], y_codes[:, part].bitcast(I32))
        for q in range(4):
            queue = nc.sync if q % 2 else nc.scalar
            queue.dma_start(out_2[0, 4 * q : 4 * q + 4, :].bitcast(I32), y_scales[32 * q : 32 * q + 4, :].bitcast(I32))
